import numpy as np
import ml_dtypes


def mxq(x, axis, fmt="e4m3"):
    dtype, down = {"e4m3": (ml_dtypes.float8_e4m3fn, 7), "e5m2": (ml_dtypes.float8_e5m2, 14)}[fmt]
    v = np.moveaxis(np.asarray(x, np.float32).astype(ml_dtypes.bfloat16).astype(np.float64), axis, -1)
    blocks = v.reshape(v.shape[:-1] + (-1, 32))
    amax = np.abs(blocks).max(-1, keepdims=True)
    byte = np.maximum(np.where(amax > 0, np.frexp(amax)[1] - 1 + 127, 0) - down, 1)
    scale = np.exp2(byte - 127.0)
    codes = (blocks / scale).astype(np.float32).astype(dtype).astype(np.float64)
    return np.moveaxis((codes * scale).reshape(v.shape), -1, axis)


WIDE = False


def mx_kscale(k):
    if not WIDE:
        return np.ones(k)
    levels = np.array([10, -10, 5, -5, 0])
    if k % 512:
        return np.exp2(np.random.permutation(np.resize(levels, k // 32))).repeat(32)
    a = np.empty((k // 512, 16))
    for p in range(k // 512):
        a[p, :8] = np.random.permutation(np.resize(levels, 8))
        for g in range(8):
            far = levels[np.abs(levels - a[p, g]) >= 10]
            a[p, g + 8] = far[np.random.randint(len(far))]
    return np.exp2(a.ravel()).repeat(32)


def f64(x):
    return np.asarray(x).astype(np.float64)


def striped(idx):
    return np.tile(idx.reshape(-1, 16).T, (8, 1)).astype(np.uint16)


def unstriped(offs):
    return offs[:16].T.reshape(-1).astype(np.int64)


def striped8(idx):
    return np.concatenate([x.reshape(-1, 16).T for x in idx]).astype(np.uint16)


def runs(offs, k):
    lists = np.stack([offs[16 * r : 16 * r + 16].T.reshape(-1) for r in range(8)]).astype(np.int64)
    return lists[np.arange(k) % 512 // 64]


def pack_weight(w):
    k, n = w.shape
    w = f64(np.asarray(w, np.float32).astype(ml_dtypes.bfloat16)).reshape(k // 32, 32, n)
    amax = np.abs(w).max(1)
    byte = np.clip(np.where(amax > 0, np.frexp(amax)[1] - 1 + 127 - 7, 1), 1, 254)
    scaled = (w * np.exp2(127.0 - byte)[:, None, :]).reshape(k, n).astype(np.float32)
    words = np.ascontiguousarray(scaled.reshape(k // 512, 128, 4, n).transpose(0, 1, 3, 2)).astype(ml_dtypes.float8_e4m3fn).view(np.uint8)
    return words, np.ascontiguousarray(byte.astype(np.uint8).reshape(k // 512, 16, n))


def unpack_weight(words, scales):
    g, p, n, _ = words.shape
    vals = np.ascontiguousarray(words).view(ml_dtypes.float8_e4m3fn).astype(np.float64) * np.repeat(np.exp2(scales.astype(np.float64) - 127.0), 8, axis=1)[..., None]
    return vals.transpose(0, 1, 3, 2).reshape(g * 512, n)

def planes(y):
    n, m = y.shape
    v = y.astype(np.float32).astype(ml_dtypes.bfloat16).astype(np.float64).reshape(n // 32, 32, m)
    top = np.abs(v).max(1)
    byte = np.clip(np.where(top > 0, np.frexp(top)[1] - 1 + 127 - 7, 1), 1, 254)
    codes = (v * np.exp2(127.0 - byte)[:, None, :]).reshape(n, m).astype(np.float32).astype(ml_dtypes.float8_e4m3fn).view(np.uint8)
    words = codes.reshape(n // 512, 128, 4, m).transpose(0, 1, 3, 2)
    return np.ascontiguousarray(words), np.ascontiguousarray(byte.astype(np.uint8).reshape(n // 512, 16, m))


K, T, S, H, G = 512, 1024, 512, 512, 2048


def setup_inputs():
    n = np.random.standard_normal
    s = mx_kscale(K)[:, None]
    packed_xT = pack_weight(n((K, T)) * s)
    packed_w1 = pack_weight(n((K, H)) / np.sqrt(K) / s)
    packed_w2 = pack_weight(n((K, H)) / np.sqrt(K) / s)
    packed_dT = pack_weight(n((K, G)) / s)
    return {
        "x_words": packed_xT[0],
        "x_scales": packed_xT[1],
        "w1_words": packed_w1[0],
        "w1_scales": packed_w1[1],
        "w2_words": packed_w2[0],
        "w2_scales": packed_w2[1],
        "gs": (np.random.uniform(0.5, 1.5, (K, 1)) * s).astype(np.float32),
        "d_words": packed_dT[0],
        "d_scales": packed_dT[1],
        "offs": striped(np.random.permutation(T)[:S]),
        "two": striped(np.random.permutation(T)[:S]),
        "n1": striped8(np.stack([np.random.permutation(S) for _ in range(8)])),
        "n2": striped8(np.stack([np.random.permutation(S) for _ in range(8)])),
        "n3": striped8(np.stack([np.random.permutation(S) for _ in range(8)])),
        "n4": striped8(np.stack([np.random.permutation(S) for _ in range(8)])),
        "k1": striped8(np.random.randint(0, G, (8, H))),
        "n5": striped8(np.stack([np.random.permutation(S) for _ in range(8)])),
        "n6": striped8(np.stack([np.random.permutation(S) for _ in range(8)])),
        "n7": striped8(np.stack([np.random.permutation(S) for _ in range(8)])),
        "n8": striped8(np.stack([np.random.permutation(S) for _ in range(8)])),
    }


def reference(x_words, x_scales, w1_words, w1_scales, w2_words, w2_scales, gs, d_words, d_scales, offs, two, n1, n2, n3, n4, k1, n5, n6, n7, n8):
    d_k1 = unpack_weight(d_words, d_scales)[np.arange(K)[:, None], runs(k1, K)]
    xq = unpack_weight(x_words, x_scales)[:, unstriped(offs)]
    y = unpack_weight(w1_words, w1_scales).T @ xq
    x_two = unpack_weight(x_words, x_scales)[:, unstriped(two)]
    d = unpack_weight(w2_words, w2_scales).T @ x_two
    z = f64(gs) * (np.maximum(y[np.arange(H)[:, None], runs(n1, H)] + d[np.arange(H)[:, None], runs(n3, H)], y[np.arange(H)[:, None], runs(n2, H)] + d[np.arange(H)[:, None], runs(n4, H)]))
    h = 0.0625 * ((d_k1.T @ mxq(z, 0, "e4m3")))
    out_0 = 0.75 * ((h[np.arange(H)[:, None], runs(n5, H)]) * (h[np.arange(H)[:, None], runs(n6, H)]) - ((h[np.arange(H)[:, None], runs(n7, H)]) * (h[np.arange(H)[:, None], runs(n8, H)])))
    return (out_0,) + planes(out_0)

@@ -1,0 +1,209 @@
+import math
+from contextlib import ExitStack
+
+import concourse.mybir as mybir
+
+K, T, S, H, G = 512, 1024, 512, 512, 2048
+FLOPS = 3 * 2 * K * H * S
+
+F32 = mybir.dt.float32
+BF16 = mybir.dt.bfloat16
+I32 = mybir.dt.int32
+U32 = mybir.dt.uint32
+U16 = mybir.dt.uint16
+U8 = mybir.dt.uint8
+FP8X4 = mybir.dt.float8_e4m3fn_x4
+ALU = mybir.AluOpType
+ACT = mybir.ActivationFunctionType
+
+P = 128
+PACK = 4
+H_SCALE = 0.0625 * math.sqrt(0.75)
+Z_CHUNKS = (128, 256, 128)
+OUT_CHUNKS = (256, 128, 128)
+
+
+def spans(widths):
+    starts = [sum(widths[:i]) for i in range(len(widths))]
+    return [(s, s + w) for s, w in zip(starts, widths)]
+
+
+def as_words(dram):
+    return dram[0].rearrange("p n r -> p (n r)").bitcast(I32)
+
+
+def tile_picked_twqpathbdet_none_po_kernel(
+    tc, x_words, x_scales, w1_words, w1_scales, w2_words, w2_scales, gs, d_words, d_scales,
+    offs, two, n1, n2, n3, n4, k1, n5, n6, n7, n8, out_0, out_1, out_2,
+):
+    nc = tc.nc
+    with ExitStack() as ctx:
+        lists = ctx.enter_context(tc.tile_pool(name="lists", bufs=1))
+        keep = ctx.enter_context(tc.tile_pool(name="keep", bufs=1))
+        psum = ctx.enter_context(tc.psum_pool(name="psum", bufs=1))
+
+        def load_list(dram, name):
+            t = lists.tile([P, S // 16], U16, name=name)
+            nc.sync.dma_start(t[:], dram)
+            return t
+
+        def sb(shape, dtype, name):
+            return keep.tile(shape, dtype, name=name, align_bytes=64)
+
+        x_byte_table = sb([P, T], U8, "x_byte_table")
+        w_bytes = sb([P, H], U8, "w_bytes")
+        d_byte_table = sb([P, G], U8, "d_byte_table")
+        dk_plane = sb([P, H], U8, "dk_plane")
+        nc.gpsimd.memset(x_byte_table[:].bitcast(I32), 0)
+        nc.gpsimd.memset(w_bytes[:].bitcast(I32), 0)
+        nc.vector.memset(d_byte_table[:].bitcast(I32), 0)
+        nc.vector.memset(dk_plane[:].bitcast(I32), 0)
+
+        x_word_table = sb([P, T], I32, "x_word_table")
+        nc.sync.dma_start(x_word_table[:], as_words(x_words))
+        offs_l = load_list(offs, "offs_l")
+        for q in range(4):
+            nc.sync.dma_start(x_byte_table[32 * q : 32 * q + 4, :].bitcast(I32), x_scales[0, 4 * q : 4 * q + 4, :].bitcast(I32))
+        w1_raw = sb([P, H], I32, "w1_raw")
+        nc.sync.dma_start(w1_raw[:], as_words(w1_words))
+        for q in range(4):
+            nc.sync.dma_start(w_bytes[32 * q : 32 * q + 4, :].bitcast(I32), w1_scales[0, 4 * q : 4 * q + 4, :].bitcast(I32))
+        for q in range(4):
+            nc.sync.dma_start(w_bytes[32 * q + 4 : 32 * q + 8, :].bitcast(I32), w2_scales[0, 4 * q : 4 * q + 4, :].bitcast(I32))
+        two_l = load_list(two, "two_l")
+        gain = sb([P, PACK], F32, "gain")
+        nc.gpsimd.dma_start(gain[:], gs.rearrange("(p t) o -> p (t o)", t=PACK))
+        nc.gpsimd.dma_start(d_byte_table[0:P:8, :].bitcast(I32), d_scales[0].bitcast(I32))
+        w2_raw = sb([P, H], I32, "w2_raw")
+        nc.sync.dma_start(w2_raw[:], as_words(w2_words))
+        n1_l = load_list(n1, "n1_l")
+        n2_l = load_list(n2, "n2_l")
+        k1_l = load_list(k1, "k1_l")
+        d_word_table = sb([P, G], I32, "d_word_table")
+        nc.sync.dma_start(d_word_table[:], as_words(d_words))
+        n3_l = load_list(n3, "n3_l")
+        n4_l = load_list(n4, "n4_l")
+        n5_l = load_list(n5, "n5_l")
+        n6_l = load_list(n6, "n6_l")
+        n7_l = load_list(n7, "n7_l")
+        n8_l = load_list(n8, "n8_l")
+
+        def deal(copy, out, in_):
+            copy(out.rearrange("p (t m) -> p m t", t=PACK), in_.rearrange("p (m t) -> p m t", t=PACK))
+
+        w1_dealt = sb([P, H], U32, "w1_dealt")
+        w2_dealt = sb([P, H], U32, "w2_dealt")
+        deal(nc.scalar.copy, w1_dealt[:], w1_raw[:].bitcast(U32))
+        gain_abs = sb([P, PACK], F32, "gain_abs")
+        nc.scalar.activation(gain_abs[:], gain[:], ACT.Abs)
+        deal(nc.scalar.copy, w2_dealt[:], w2_raw[:].bitcast(U32))
+        widest = max(Z_CHUNKS)
+        gain_sign = sb([P, widest, PACK], BF16, "gain_sign")
+        nc.scalar.activation(gain_sign[:], gain[:].unsqueeze(1).to_broadcast([P, widest, PACK]), ACT.Sign)
+
+        def pick(table, lst, dtype, name):
+            got = sb([P, S], dtype, name)
+            nc.vector.tensor_copy(got[:], table[:].bitcast(dtype).indirect(lst[:]))
+            return got
+
+        x1_plane = pick(x_byte_table, offs_l, U8, "x1_plane")
+        x1_words = pick(x_word_table, offs_l, U32, "x1_words")
+        w_planes = sb([P, H], U8, "w_planes")
+        nc.vector.tensor_copy(w_planes[:].rearrange("p (t m) -> p t m", t=PACK), w_bytes[:].rearrange("p (m t) -> p t m", t=PACK))
+        x2_plane = pick(x_byte_table, two_l, U8, "x2_plane")
+        x2_words = pick(x_word_table, two_l, U32, "x2_words")
+
+        def product(bank, cols, t, w_words, w_plane, words, plane):
+            rows = slice(P * t, P * (t + 1))
+            nc.tensor.matmul_mx(
+                out=bank[:, cols], lhsT=w_words[:, rows].bitcast(FP8X4), lhsT_scale=w_plane[:, rows],
+                rhs=words[:, cols].bitcast(FP8X4), rhs_scale=plane[:, cols], start=True, stop=True,
+            )
+
+        everything = slice(0, S)
+        y_banks = [psum.tile([P, S], F32, name="bank%d" % t) for t in range(PACK)]
+        d_banks = [psum.tile([P, S], F32, name="bank%d" % (PACK + t)) for t in range(PACK)]
+        for t in range(PACK):
+            product(y_banks[t], everything, t, w1_dealt, w_planes[0:P], x1_words, x1_plane)
+        for t in range(PACK):
+            product(d_banks[t], everything, t, w2_dealt, w_planes[4:P], x2_words, x2_plane)
+
+        dk_words = pick(d_word_table, k1_l, U32, "dk_words")
+        dk_bytes = pick(d_byte_table, k1_l, U8, "dk_bytes")
+        dk_dealt = sb([P, H], U32, "dk_dealt")
+        deal(nc.vector.tensor_copy, dk_dealt[:], dk_words[:])
+        dk_bytes_dealt = sb([P, H], U8, "dk_bytes_dealt")
+        nc.vector.tensor_copy(dk_bytes_dealt[:].rearrange("p (t m) -> p t m", t=PACK), dk_bytes[:].rearrange("p (m t) -> p t m", t=PACK))
+        for r in range(4):
+            nc.sync.dma_start(dk_plane[r:P:32, :].bitcast(I32), dk_bytes_dealt[8 * r : P : 32, :].bitcast(I32))
+
+        y = [sb([P, S], F32, "y%d" % t) for t in range(PACK)]
+        d = [sb([P, S], F32, "d%d" % t) for t in range(PACK)]
+        h = [sb([P, S], F32, "h%d" % t) for t in range(PACK)]
+
+        def at(window, lst, lo, hi):
+            return window[:].indirect(lst[:, lo // 16 : hi // 16])
+
+        def fetch(out, window, lst, lo, hi):
+            nc.scalar.activation(out, at(window, lst, lo, hi), ACT.Copy)
+
+        def woven(ap):
+            return ap.rearrange("p (c i t) -> p c t i", i=4, t=PACK)
+
+        def by_plane(ap):
+            return ap.rearrange("p t (c i) -> p c t i", i=4)
+
+        z_words = sb([P, S], U32, "z_words")
+        z_plane = sb([P, S], U8, "z_plane")
+        h_banks = [psum.tile([P, S], F32, name="bank%d" % t) for t in range(PACK)]
+        for n, (lo, hi) in enumerate(spans(Z_CHUNKS)):
+            w = hi - lo
+            ya = sb([P, PACK, w], F32, "ya%d" % n)
+            yb = sb([P, PACK, w], F32, "yb%d" % n)
+            a = sb([P, PACK, w], F32, "a%d" % n)
+            b = sb([P, PACK, w], F32, "b%d" % n)
+            for t in range(PACK):
+                if n == 0:
+                    nc.scalar.activation(y[t][:], y_banks[t][:], ACT.Copy, scale=gain_abs[:, t : t + 1])
+                fetch(ya[:, t, :], y[t], n1_l, lo, hi)
+                fetch(yb[:, t, :], y[t], n2_l, lo, hi)
+                if n == 0:
+                    nc.scalar.activation(d[t][:], d_banks[t][:], ACT.Copy, scale=gain_abs[:, t : t + 1])
+                nc.vector.tensor_tensor(a[:, t, :], at(d[t], n3_l, lo, hi), ya[:, t, :], ALU.add)
+                nc.vector.tensor_tensor(b[:, t, :], at(d[t], n4_l, lo, hi), yb[:, t, :], ALU.add)
+            z_abs = sb([P, PACK * w], BF16, "z_abs%d" % n)
+            nc.vector.tensor_tensor(woven(z_abs[:]), by_plane(a[:]), by_plane(b[:]), ALU.max)
+            z = sb([P, PACK * w], BF16, "z%d" % n)
+            nc.vector.tensor_tensor(z[:], z_abs[:], gain_sign[:, 0:w, :].rearrange("p c t -> p (c t)"), ALU.mult)
+            nc.vector.quantize_mx(z_words[:, lo:hi].bitcast(FP8X4), z_plane[:, lo:hi], z[:])
+            for t in range(PACK):
+                product(h_banks[t], slice(lo, hi), t, dk_dealt, dk_plane, z_words, z_plane)
+                nc.scalar.activation(h[t][:, lo:hi], h_banks[t][:, lo:hi], ACT.Copy, scale=H_SCALE)
+
+        out_rows = out_0.rearrange("(p t) j -> p t j", t=PACK)
+        out_words = sb([P, S], I32, "out_words")
+        out_plane = sb([P, S], U8, "out_plane")
+        for n, (lo, hi) in enumerate(spans(OUT_CHUNKS)):
+            w = hi - lo
+            h5 = sb([P, PACK, w], F32, "h5_%d" % n)
+            h7 = sb([P, PACK, w], F32, "h7_%d" % n)
+            p1 = sb([P, PACK, w], F32, "p1_%d" % n)
+            p2 = sb([P, PACK, w], F32, "p2_%d" % n)
+            for t in range(PACK):
+                fetch(h5[:, t, :], h[t], n5_l, lo, hi)
+                if n == 0 and t == 0:
+                    nc.vector.tensor_copy(h7[:, t, :], at(h[t], n7_l, lo, hi))
+                else:
+                    fetch(h7[:, t, :], h[t], n7_l, lo, hi)
+                nc.vector.tensor_tensor(p1[:, t, :], at(h[t], n6_l, lo, hi), h5[:, t, :], ALU.mult)
+                nc.vector.tensor_tensor(p2[:, t, :], at(h[t], n8_l, lo, hi), h7[:, t, :], ALU.mult)
+            res = sb([P, PACK, w], F32, "res%d" % n)
+            nc.vector.tensor_tensor(res[:], p1[:], p2[:], ALU.subtract)
+            nc.sync.dma_start(out_rows[:, :, lo:hi], res[:])
+            rounded = sb([P, PACK * w], BF16, "rounded%d" % n)
+            weave = nc.vector.tensor_copy if hi == S else nc.scalar.copy
+            weave(woven(rounded[:]), by_plane(res[:]))
+            nc.vector.quantize_mx(out_words[:, lo:hi].bitcast(FP8X4), out_plane[:, lo:hi], rounded[:])
+            nc.sync.dma_start(as_words(out_1)[:, lo:hi], out_words[:, lo:hi])
+        for q in range(4):
+            nc.scalar.dma_start(out_2[0, 4 * q : 4 * q + 4, :].bitcast(I32), out_plane[32 * q : 32 * q + 4, :].bitcast(I32))

@@ -19,13 +19,10 @@ ACT = mybir.ActivationFunctionType
 P = 128
 PACK = 4
 H_SCALE = 0.0625 * math.sqrt(0.75)
-Z_CHUNKS = (128, 256, 128)
-OUT_CHUNKS = (256, 128, 128)
-
-
-def spans(widths):
-    starts = [sum(widths[:i]) for i in range(len(widths))]
-    return [(s, s + w) for s, w in zip(starts, widths)]
+HALF = S // 2
+LAST = PACK - 1
+P1 = {"chunks":[256,128,128],"kinds":[[[0,1,2]],[[0,1,2]],[[0],[1,2]],[[0],[1],[2]]],"unf":{"2,1":2,"3,1":2},"vev":[0]}
+P2 = {"chunks":[256,128,128],"kinds":[[[0,1,2]],[[0,1,2]],[[0],[1,2]],[[0],[1],[2]]],"unf":{"2,1":2,"3,1":2,"3,2":2},"ilS":[0,2],"vplain":[[0,0]]}
 
 
 def as_words(dram):
@@ -47,8 +44,8 @@ def tile_picked_twqpathbdet_none_po_kernel(
             nc.sync.dma_start(t[:], dram)
             return t
 
-        def sb(shape, dtype, name):
-            return keep.tile(shape, dtype, name=name, align_bytes=64)
+        def sb(shape, dtype, name, tag=None):
+            return keep.tile(shape, dtype, name=name, tag=tag or name, align_bytes=64)
 
         x_byte_table = sb([P, T], U8, "x_byte_table")
         w_bytes = sb([P, H], U8, "w_bytes")
@@ -76,11 +73,11 @@ def tile_picked_twqpathbdet_none_po_kernel(
         nc.gpsimd.dma_start(d_byte_table[0:P:8, :].bitcast(I32), d_scales[0].bitcast(I32))
         w2_raw = sb([P, H], I32, "w2_raw")
         nc.sync.dma_start(w2_raw[:], as_words(w2_words))
-        n1_l = load_list(n1, "n1_l")
-        n2_l = load_list(n2, "n2_l")
         k1_l = load_list(k1, "k1_l")
         d_word_table = sb([P, G], I32, "d_word_table")
         nc.sync.dma_start(d_word_table[:], as_words(d_words))
+        n1_l = load_list(n1, "n1_l")
+        n2_l = load_list(n2, "n2_l")
         n3_l = load_list(n3, "n3_l")
         n4_l = load_list(n4, "n4_l")
         n5_l = load_list(n5, "n5_l")
@@ -97,9 +94,8 @@ def tile_picked_twqpathbdet_none_po_kernel(
         gain_abs = sb([P, PACK], F32, "gain_abs")
         nc.scalar.activation(gain_abs[:], gain[:], ACT.Abs)
         deal(nc.scalar.copy, w2_dealt[:], w2_raw[:].bitcast(U32))
-        widest = max(Z_CHUNKS)
-        gain_sign = sb([P, widest, PACK], BF16, "gain_sign")
-        nc.scalar.activation(gain_sign[:], gain[:].unsqueeze(1).to_broadcast([P, widest, PACK]), ACT.Sign)
+        gain_sign = sb([P, HALF, PACK], BF16, "gain_sign")
+        nc.scalar.activation(gain_sign[:], gain[:].unsqueeze(1).to_broadcast([P, HALF, PACK]), ACT.Sign)
 
         def pick(table, lst, dtype, name):
             got = sb([P, S], dtype, name)
@@ -137,15 +133,32 @@ def tile_picked_twqpathbdet_none_po_kernel(
         for r in range(4):
             nc.sync.dma_start(dk_plane[r:P:32, :].bitcast(I32), dk_bytes_dealt[8 * r : P : 32, :].bitcast(I32))
 
-        y = [sb([P, S], F32, "y%d" % t) for t in range(PACK)]
-        d = [sb([P, S], F32, "d%d" % t) for t in range(PACK)]
-        h = [sb([P, S], F32, "h%d" % t) for t in range(PACK)]
+        def window(name, narrow):
+            return sb([P, S if narrow else 2 * S], F32, name)
 
-        def at(window, lst, lo, hi):
-            return window[:].indirect(lst[:, lo // 16 : hi // 16])
+        def bounds(chunks):
+            return [sum(chunks[:i]) for i in range(len(chunks) + 1)]
 
-        def fetch(out, window, lst, lo, hi):
-            nc.scalar.activation(out, at(window, lst, lo, hi), ACT.Copy)
+        def plan(spec):
+            edge = bounds(spec["chunks"])
+            items = []
+            for t in range(PACK):
+                for grp in spec["kinds"][t]:
+                    items.append((grp[0], t, slice(edge[grp[0]], edge[grp[-1] + 1])))
+            return sorted(items, key=lambda it: (it[0], it[1]))
+
+        def narrow(spec, t):
+            return any(c.stop - c.start < HALF for g, tt, c in plan(spec) if tt == t)
+
+        y = [window("y%d" % t, narrow(P1, t)) for t in range(PACK)]
+        d = [window("d%d" % t, narrow(P1, t)) for t in range(PACK)]
+        h = [window("h%d" % t, narrow(P2, t)) for t in range(PACK)]
+
+        def at(win, lst, cols):
+            return win[:].indirect(lst[:, cols.start // 16 : cols.stop // 16])
+
+        def fetch(out, win, lst, cols):
+            nc.scalar.activation(out, at(win, lst, cols), ACT.Copy)
 
         def woven(ap):
             return ap.rearrange("p (c i t) -> p c t i", i=4, t=PACK)
@@ -153,57 +166,94 @@ def tile_picked_twqpathbdet_none_po_kernel(
         def by_plane(ap):
             return ap.rearrange("p t (c i) -> p c t i", i=4)
 
+        def pair(spec, g, t, cols, left, right, lists4, got, other, both, op, between=None):
+            how = spec["unf"].get("%d,%d" % (t, g), 0)
+            fetch(got[:, 0, t, cols], left, lists4[0], cols)
+            if between:
+                between()
+            if [t, g] in spec.get("vplain", []):
+                nc.vector.tensor_copy(got[:, 1, t, cols], at(left, lists4[1], cols))
+            else:
+                fetch(got[:, 1, t, cols], left, lists4[1], cols)
+            if how == 2:
+                fetch(other[:, 0, t, cols], right, lists4[2], cols)
+                fetch(other[:, 1, t, cols], right, lists4[3], cols)
+                nc.vector.tensor_tensor(both[:, :, t, cols], got[:, :, t, cols], other[:, :, t, cols], op)
+            else:
+                if how == 1:
+                    fetch(other[:, 1, t, cols], right, lists4[3], cols)
+                nc.vector.tensor_tensor(both[:, 0, t, cols], at(right, lists4[2], cols), got[:, 0, t, cols], op)
+                if how == 1:
+                    nc.vector.tensor_tensor(both[:, 1, t, cols], other[:, 1, t, cols], got[:, 1, t, cols], op)
+                else:
+                    nc.vector.tensor_tensor(both[:, 1, t, cols], at(right, lists4[3], cols), got[:, 1, t, cols], op)
+
         z_words = sb([P, S], U32, "z_words")
         z_plane = sb([P, S], U8, "z_plane")
-        h_banks = [psum.tile([P, S], F32, name="bank%d" % t) for t in range(PACK)]
-        for n, (lo, hi) in enumerate(spans(Z_CHUNKS)):
-            w = hi - lo
-            ya = sb([P, PACK, w], F32, "ya%d" % n)
-            yb = sb([P, PACK, w], F32, "yb%d" % n)
-            a = sb([P, PACK, w], F32, "a%d" % n)
-            b = sb([P, PACK, w], F32, "b%d" % n)
-            for t in range(PACK):
-                if n == 0:
-                    nc.scalar.activation(y[t][:], y_banks[t][:], ACT.Copy, scale=gain_abs[:, t : t + 1])
-                fetch(ya[:, t, :], y[t], n1_l, lo, hi)
-                fetch(yb[:, t, :], y[t], n2_l, lo, hi)
-                if n == 0:
-                    nc.scalar.activation(d[t][:], d_banks[t][:], ACT.Copy, scale=gain_abs[:, t : t + 1])
-                nc.vector.tensor_tensor(a[:, t, :], at(d[t], n3_l, lo, hi), ya[:, t, :], ALU.add)
-                nc.vector.tensor_tensor(b[:, t, :], at(d[t], n4_l, lo, hi), yb[:, t, :], ALU.add)
-            z_abs = sb([P, PACK * w], BF16, "z_abs%d" % n)
-            nc.vector.tensor_tensor(woven(z_abs[:]), by_plane(a[:]), by_plane(b[:]), ALU.max)
-            z = sb([P, PACK * w], BF16, "z%d" % n)
+        y_at = sb([P, 2, PACK, S], F32, "y_at")
+        d_at = sb([P, 2, PACK, S], F32, "d_at")
+        sums = sb([P, 2, PACK, S], F32, "sums")
+
+        def empty(win, bank, t, on_vector):
+            if on_vector:
+                nc.vector.tensor_scalar_mul(win[:, 0:S], bank[:], gain_abs[:, t : t + 1])
+            else:
+                nc.scalar.activation(win[:, 0:S], bank[:], ACT.Copy, scale=gain_abs[:, t : t + 1])
+
+        def make_h(g):
+            edge = bounds(P1["chunks"])
+            cols = slice(edge[g], edge[g + 1])
+            w = cols.stop - cols.start
+            z_abs = sb([P, PACK * w], BF16, "z_abs_%d" % g)
+            nc.vector.tensor_tensor(woven(z_abs[:]), by_plane(sums[:, 0, :, cols]), by_plane(sums[:, 1, :, cols]), ALU.max)
+            z = sb([P, PACK * w], BF16, "z_%d" % g)
             nc.vector.tensor_tensor(z[:], z_abs[:], gain_sign[:, 0:w, :].rearrange("p c t -> p (c t)"), ALU.mult)
-            nc.vector.quantize_mx(z_words[:, lo:hi].bitcast(FP8X4), z_plane[:, lo:hi], z[:])
+            nc.vector.quantize_mx(z_words[:, cols].bitcast(FP8X4), z_plane[:, cols], z[:])
             for t in range(PACK):
-                product(h_banks[t], slice(lo, hi), t, dk_dealt, dk_plane, z_words, z_plane)
-                nc.scalar.activation(h[t][:, lo:hi], h_banks[t][:, lo:hi], ACT.Copy, scale=H_SCALE)
+                bank = psum.tile([P, S], F32, name="bank%d" % (t + PACK * (g % 2)))
+                product(bank, cols, t, dk_dealt, dk_plane, z_words, z_plane)
+                if cols.stop == S and t > 0:
+                    nc.vector.tensor_scalar_mul(h[t][:, cols], bank[:, cols], H_SCALE)
+                else:
+                    nc.scalar.activation(h[t][:, cols], bank[:, cols], ACT.Copy, scale=H_SCALE)
+
+        done = 0
+        empty(y[0], y_banks[0], 0, False)
+        for g, t, cols in plan(P1):
+            for k in range(done, g):
+                make_h(k)
+            done = g
+            if g == 0:
+                if t > 0:
+                    empty(y[t], y_banks[t], t, False)
+            between = (lambda: empty(d[t], d_banks[t], t, t in P1["vev"])) if g == 0 else None
+            pair(P1, g, t, cols, y[t], d[t], (n1_l, n2_l, n3_l, n4_l), y_at, d_at, sums, ALU.add, between)
+        for k in range(done, len(P1["chunks"])):
+            make_h(k)
 
         out_rows = out_0.rearrange("(p t) j -> p t j", t=PACK)
         out_words = sb([P, S], I32, "out_words")
         out_plane = sb([P, S], U8, "out_plane")
-        for n, (lo, hi) in enumerate(spans(OUT_CHUNKS)):
-            w = hi - lo
-            h5 = sb([P, PACK, w], F32, "h5_%d" % n)
-            h7 = sb([P, PACK, w], F32, "h7_%d" % n)
-            p1 = sb([P, PACK, w], F32, "p1_%d" % n)
-            p2 = sb([P, PACK, w], F32, "p2_%d" % n)
-            for t in range(PACK):
-                fetch(h5[:, t, :], h[t], n5_l, lo, hi)
-                if n == 0 and t == 0:
-                    nc.vector.tensor_copy(h7[:, t, :], at(h[t], n7_l, lo, hi))
-                else:
-                    fetch(h7[:, t, :], h[t], n7_l, lo, hi)
-                nc.vector.tensor_tensor(p1[:, t, :], at(h[t], n6_l, lo, hi), h5[:, t, :], ALU.mult)
-                nc.vector.tensor_tensor(p2[:, t, :], at(h[t], n8_l, lo, hi), h7[:, t, :], ALU.mult)
-            res = sb([P, PACK, w], F32, "res%d" % n)
-            nc.vector.tensor_tensor(res[:], p1[:], p2[:], ALU.subtract)
-            nc.sync.dma_start(out_rows[:, :, lo:hi], res[:])
-            rounded = sb([P, PACK * w], BF16, "rounded%d" % n)
-            weave = nc.vector.tensor_copy if hi == S else nc.scalar.copy
-            weave(woven(rounded[:]), by_plane(res[:]))
-            nc.vector.quantize_mx(out_words[:, lo:hi].bitcast(FP8X4), out_plane[:, lo:hi], rounded[:])
-            nc.sync.dma_start(as_words(out_1)[:, lo:hi], out_words[:, lo:hi])
+        h_at = sb([P, 2, PACK, S], F32, "h_at", "y_at")
+        h_other = sb([P, 2, PACK, S], F32, "h_other", "d_at")
+        prods = sb([P, 2, PACK, S], F32, "prods")
+        res = sb([P, PACK, S], F32, "res")
+
+        def hand_on(g):
+            edge = bounds(P2["chunks"])
+            cols = slice(edge[g], edge[g + 1])
+            w = cols.stop - cols.start
+            rounded = sb([P, PACK * w], BF16, "rounded_%d" % g)
+            weave = nc.scalar.copy if g in P2["ilS"] else nc.vector.tensor_copy
+            weave(woven(rounded[:]), by_plane(res[:, :, cols]))
+            nc.vector.quantize_mx(out_words[:, cols].bitcast(FP8X4), out_plane[:, cols], rounded[:])
+            nc.sync.dma_start(as_words(out_1)[:, cols], out_words[:, cols])
+
+        for g, t, cols in plan(P2):
+            pair(P2, g, t, cols, h[t], h[t], (n5_l, n7_l, n6_l, n8_l), h_at, h_other, prods, ALU.mult)
+            nc.vector.tensor_tensor(res[:, t, cols], prods[:, 0, t, cols], prods[:, 1, t, cols], ALU.subtract)
+            nc.sync.dma_start(out_rows[:, t, cols], res[:, t, cols])
+        for k in range(len(P2["chunks"])):
+            hand_on(k)
         for q in range(4):
-            nc.scalar.dma_start(out_2[0, 4 * q : 4 * q + 4, :].bitcast(I32), out_plane[32 * q : 32 * q + 4, :].bitcast(I32))
+            (nc.scalar if q % 2 else nc.sync).dma_start(out_2[0, 4 * q : 4 * q + 4, :].bitcast(I32), out_plane[32 * q : 32 * q + 4, :].bitcast(I32))

@@ -18,15 +18,34 @@ ACT = mybir.ActivationFunctionType
 
 P = 128
 PACK = 4
+QUADRANTS = 4
+LIST_GROUP = 16
+WEAVE_RUN = 4
 H_SCALE = 0.0625 * math.sqrt(0.75)
-HALF = S // 2
-LAST = PACK - 1
-P1 = {"chunks":[256,128,128],"kinds":[[[0,1,2]],[[0,1,2]],[[0],[1,2]],[[0],[1],[2]]],"unf":{"2,1":2,"3,1":2},"vev":[0]}
-P2 = {"chunks":[256,128,128],"kinds":[[[0,1,2]],[[0,1,2]],[[0],[1,2]],[[0],[1],[2]]],"unf":{"2,1":2,"3,1":2,"3,2":2},"ilS":[0,2],"vplain":[[0,0]]}
+
+ALL = slice(0, S)
+FIRST_HALF = slice(0, S // 2)
+SECOND_HALF = slice(S // 2, S)
+THIRD_QUARTER = slice(S // 2, 3 * S // 4)
+LAST_QUARTER = slice(3 * S // 4, S)
+WHOLE_TILES = 2
+LAST_TILE = PACK - 1
+
+
+def width(cols):
+    return cols.stop - cols.start
 
 
 def as_words(dram):
     return dram[0].rearrange("p n r -> p (n r)").bitcast(I32)
+
+
+def woven(ap):
+    return ap.rearrange("p (c i t) -> p c t i", i=WEAVE_RUN, t=PACK)
+
+
+def by_row_tile(ap):
+    return ap.rearrange("p t (c i) -> p c t i", i=WEAVE_RUN)
 
 
 def tile_picked_twqpathbdet_none_po_kernel(
@@ -39,221 +58,223 @@ def tile_picked_twqpathbdet_none_po_kernel(
         keep = ctx.enter_context(tc.tile_pool(name="keep", bufs=1))
         psum = ctx.enter_context(tc.psum_pool(name="psum", bufs=1))
 
-        def load_list(dram, name):
-            t = lists.tile([P, S // 16], U16, name=name)
-            nc.sync.dma_start(t[:], dram)
-            return t
+        def sb(shape, dtype, name):
+            return keep.tile(shape, dtype, name=name, align_bytes=64)
 
-        def sb(shape, dtype, name, tag=None):
-            return keep.tile(shape, dtype, name=name, tag=tag or name, align_bytes=64)
+        def bank_tile(number):
+            return psum.tile([P, S], F32, name="bank%d" % number)
 
         x_byte_table = sb([P, T], U8, "x_byte_table")
-        w_bytes = sb([P, H], U8, "w_bytes")
+        w1_bytes = sb([P, H], U8, "w1_bytes")
+        w2_bytes = sb([P, H], U8, "w2_bytes")
         d_byte_table = sb([P, G], U8, "d_byte_table")
-        dk_plane = sb([P, H], U8, "dk_plane")
-        nc.gpsimd.memset(x_byte_table[:].bitcast(I32), 0)
-        nc.gpsimd.memset(w_bytes[:].bitcast(I32), 0)
-        nc.vector.memset(d_byte_table[:].bitcast(I32), 0)
-        nc.vector.memset(dk_plane[:].bitcast(I32), 0)
+        dk_scales = sb([P, H], U8, "dk_scales")
+        for table in (x_byte_table, w1_bytes, w2_bytes):
+            nc.gpsimd.memset(table[:].bitcast(I32), 0)
+        for table in (d_byte_table, dk_scales):
+            nc.vector.memset(table[:].bitcast(I32), 0)
 
-        x_word_table = sb([P, T], I32, "x_word_table")
-        nc.sync.dma_start(x_word_table[:], as_words(x_words))
-        offs_l = load_list(offs, "offs_l")
-        for q in range(4):
-            nc.sync.dma_start(x_byte_table[32 * q : 32 * q + 4, :].bitcast(I32), x_scales[0, 4 * q : 4 * q + 4, :].bitcast(I32))
-        w1_raw = sb([P, H], I32, "w1_raw")
-        nc.sync.dma_start(w1_raw[:], as_words(w1_words))
-        for q in range(4):
-            nc.sync.dma_start(w_bytes[32 * q : 32 * q + 4, :].bitcast(I32), w1_scales[0, 4 * q : 4 * q + 4, :].bitcast(I32))
-        for q in range(4):
-            nc.sync.dma_start(w_bytes[32 * q + 4 : 32 * q + 8, :].bitcast(I32), w2_scales[0, 4 * q : 4 * q + 4, :].bitcast(I32))
-        two_l = load_list(two, "two_l")
+        def load_list(dram, name):
+            offsets = lists.tile([P, S // LIST_GROUP], U16, name=name)
+            nc.sync.dma_start(offsets[:], dram)
+            return offsets
+
+        def load_scale_rows(table, dram):
+            for q in range(QUADRANTS):
+                nc.sync.dma_start(table[32 * q : 32 * q + 4, :].bitcast(I32), dram[0, 4 * q : 4 * q + 4, :].bitcast(I32))
+
+        def load_words(dram, columns, name):
+            table = sb([P, columns], I32, name)
+            nc.sync.dma_start(table[:], as_words(dram))
+            return table
+
         gain = sb([P, PACK], F32, "gain")
         nc.gpsimd.dma_start(gain[:], gs.rearrange("(p t) o -> p (t o)", t=PACK))
         nc.gpsimd.dma_start(d_byte_table[0:P:8, :].bitcast(I32), d_scales[0].bitcast(I32))
-        w2_raw = sb([P, H], I32, "w2_raw")
-        nc.sync.dma_start(w2_raw[:], as_words(w2_words))
-        k1_l = load_list(k1, "k1_l")
-        d_word_table = sb([P, G], I32, "d_word_table")
-        nc.sync.dma_start(d_word_table[:], as_words(d_words))
-        n1_l = load_list(n1, "n1_l")
-        n2_l = load_list(n2, "n2_l")
-        n3_l = load_list(n3, "n3_l")
-        n4_l = load_list(n4, "n4_l")
-        n5_l = load_list(n5, "n5_l")
-        n6_l = load_list(n6, "n6_l")
-        n7_l = load_list(n7, "n7_l")
-        n8_l = load_list(n8, "n8_l")
+        x_word_table = load_words(x_words, T, "x_word_table")
+        offs_list = load_list(offs, "offs_list")
+        load_scale_rows(x_byte_table, x_scales)
+        w1_raw = load_words(w1_words, H, "w1_raw")
+        w2_raw = load_words(w2_words, H, "w2_raw")
+        load_scale_rows(w1_bytes, w1_scales)
+        two_list = load_list(two, "two_list")
+        n1_list = load_list(n1, "n1_list")
+        load_scale_rows(w2_bytes, w2_scales)
+        n2_list = load_list(n2, "n2_list")
+        n3_list = load_list(n3, "n3_list")
+        k1_list = load_list(k1, "k1_list")
+        n4_list = load_list(n4, "n4_list")
+        d_word_table = load_words(d_words, G, "d_word_table")
+        n5_list = load_list(n5, "n5_list")
+        n6_list = load_list(n6, "n6_list")
+        n7_list = load_list(n7, "n7_list")
+        n8_list = load_list(n8, "n8_list")
 
-        def deal(copy, out, in_):
-            copy(out.rearrange("p (t m) -> p m t", t=PACK), in_.rearrange("p (m t) -> p m t", t=PACK))
+        def deal_words(copy, words, name):
+            dealt = sb([P, H], U32, name)
+            copy(dealt[:].rearrange("p (t m) -> p m t", t=PACK), words.rearrange("p (m t) -> p m t", t=PACK))
+            return dealt
 
-        w1_dealt = sb([P, H], U32, "w1_dealt")
-        w2_dealt = sb([P, H], U32, "w2_dealt")
-        deal(nc.scalar.copy, w1_dealt[:], w1_raw[:].bitcast(U32))
-        gain_abs = sb([P, PACK], F32, "gain_abs")
-        nc.scalar.activation(gain_abs[:], gain[:], ACT.Abs)
-        deal(nc.scalar.copy, w2_dealt[:], w2_raw[:].bitcast(U32))
-        gain_sign = sb([P, HALF, PACK], BF16, "gain_sign")
-        nc.scalar.activation(gain_sign[:], gain[:].unsqueeze(1).to_broadcast([P, HALF, PACK]), ACT.Sign)
+        def deal_bytes(scale_bytes, name):
+            dealt = sb([P, H], U8, name)
+            nc.vector.tensor_copy(dealt[:].rearrange("p (t m) -> p t m", t=PACK), scale_bytes[:].rearrange("p (m t) -> p t m", t=PACK))
+            return dealt
 
-        def pick(table, lst, dtype, name):
-            got = sb([P, S], dtype, name)
-            nc.vector.tensor_copy(got[:], table[:].bitcast(dtype).indirect(lst[:]))
-            return got
+        def pick(table, offsets, dtype, name):
+            picked = sb([P, S], dtype, name)
+            nc.vector.tensor_copy(picked[:], table[:].bitcast(dtype).indirect(offsets[:]))
+            return picked
 
-        x1_plane = pick(x_byte_table, offs_l, U8, "x1_plane")
-        x1_words = pick(x_word_table, offs_l, U32, "x1_words")
-        w_planes = sb([P, H], U8, "w_planes")
-        nc.vector.tensor_copy(w_planes[:].rearrange("p (t m) -> p t m", t=PACK), w_bytes[:].rearrange("p (m t) -> p t m", t=PACK))
-        x2_plane = pick(x_byte_table, two_l, U8, "x2_plane")
-        x2_words = pick(x_word_table, two_l, U32, "x2_words")
-
-        def product(bank, cols, t, w_words, w_plane, words, plane):
+        def product(bank, cols, t, stationary, stationary_scales, moving, moving_scales):
             rows = slice(P * t, P * (t + 1))
             nc.tensor.matmul_mx(
-                out=bank[:, cols], lhsT=w_words[:, rows].bitcast(FP8X4), lhsT_scale=w_plane[:, rows],
-                rhs=words[:, cols].bitcast(FP8X4), rhs_scale=plane[:, cols], start=True, stop=True,
+                out=bank[:, cols], lhsT=stationary[:, rows].bitcast(FP8X4), lhsT_scale=stationary_scales[:, rows],
+                rhs=moving[:, cols].bitcast(FP8X4), rhs_scale=moving_scales[:, cols], start=True, stop=True,
             )
 
-        everything = slice(0, S)
-        y_banks = [psum.tile([P, S], F32, name="bank%d" % t) for t in range(PACK)]
-        d_banks = [psum.tile([P, S], F32, name="bank%d" % (PACK + t)) for t in range(PACK)]
+        w1_dealt = deal_words(nc.scalar.copy, w1_raw[:].bitcast(U32), "w1_dealt")
+        gain_abs = sb([P, PACK], F32, "gain_abs")
+        nc.scalar.activation(gain_abs[:], gain[:], ACT.Abs)
+        w2_dealt = deal_words(nc.scalar.copy, w2_raw[:].bitcast(U32), "w2_dealt")
+        gain_sign = sb([P, width(FIRST_HALF), PACK], BF16, "gain_sign")
+        nc.scalar.activation(gain_sign[:], gain[:].unsqueeze(1).to_broadcast([P, width(FIRST_HALF), PACK]), ACT.Sign)
+
+        x1_scales = pick(x_byte_table, offs_list, U8, "x1_scales")
+        x1_words = pick(x_word_table, offs_list, U32, "x1_words")
+        w1_dealt_scales = deal_bytes(w1_bytes, "w1_dealt_scales")
+        x2_scales = pick(x_byte_table, two_list, U8, "x2_scales")
+        x2_words = pick(x_word_table, two_list, U32, "x2_words")
+        y_banks = [bank_tile(t) for t in range(PACK)]
+        d_banks = [bank_tile(PACK + t) for t in range(PACK)]
         for t in range(PACK):
-            product(y_banks[t], everything, t, w1_dealt, w_planes[0:P], x1_words, x1_plane)
+            product(y_banks[t], ALL, t, w1_dealt, w1_dealt_scales, x1_words, x1_scales)
+        w2_dealt_scales = deal_bytes(w2_bytes, "w2_dealt_scales")
         for t in range(PACK):
-            product(d_banks[t], everything, t, w2_dealt, w_planes[4:P], x2_words, x2_plane)
+            product(d_banks[t], ALL, t, w2_dealt, w2_dealt_scales, x2_words, x2_scales)
+        dk_bytes = pick(d_byte_table, k1_list, U8, "dk_bytes")
 
-        dk_words = pick(d_word_table, k1_l, U32, "dk_words")
-        dk_bytes = pick(d_byte_table, k1_l, U8, "dk_bytes")
-        dk_dealt = sb([P, H], U32, "dk_dealt")
-        deal(nc.vector.tensor_copy, dk_dealt[:], dk_words[:])
-        dk_bytes_dealt = sb([P, H], U8, "dk_bytes_dealt")
-        nc.vector.tensor_copy(dk_bytes_dealt[:].rearrange("p (t m) -> p t m", t=PACK), dk_bytes[:].rearrange("p (m t) -> p t m", t=PACK))
-        for r in range(4):
-            nc.sync.dma_start(dk_plane[r:P:32, :].bitcast(I32), dk_bytes_dealt[8 * r : P : 32, :].bitcast(I32))
+        def windows(name):
+            return [sb([P, 2 * S if t < WHOLE_TILES else S], F32, "%s%d" % (name, t)) for t in range(PACK)]
 
-        def window(name, narrow):
-            return sb([P, S if narrow else 2 * S], F32, name)
+        y, d, h = windows("y"), windows("d"), windows("h")
 
-        def bounds(chunks):
-            return [sum(chunks[:i]) for i in range(len(chunks) + 1)]
+        def at(window, offsets, cols):
+            return window[:].indirect(offsets[:, cols.start // LIST_GROUP : cols.stop // LIST_GROUP])
 
-        def plan(spec):
-            edge = bounds(spec["chunks"])
-            items = []
-            for t in range(PACK):
-                for grp in spec["kinds"][t]:
-                    items.append((grp[0], t, slice(edge[grp[0]], edge[grp[-1] + 1])))
-            return sorted(items, key=lambda it: (it[0], it[1]))
+        def fetch(out, window, offsets, cols):
+            nc.scalar.activation(out, at(window, offsets, cols), ACT.Copy)
 
-        def narrow(spec, t):
-            return any(c.stop - c.start < HALF for g, tt, c in plan(spec) if tt == t)
+        def lead_cols(t):
+            return ALL if t < WHOLE_TILES else FIRST_HALF
 
-        y = [window("y%d" % t, narrow(P1, t)) for t in range(PACK)]
-        d = [window("d%d" % t, narrow(P1, t)) for t in range(PACK)]
-        h = [window("h%d" % t, narrow(P2, t)) for t in range(PACK)]
+        def combine_fused(op, result, left, right_window, right_lists, t, cols):
+            for term in range(2):
+                nc.vector.tensor_tensor(result[:, term, t, cols], at(right_window, right_lists[term], cols), left[:, term, t, cols], op)
 
-        def at(win, lst, cols):
-            return win[:].indirect(lst[:, cols.start // 16 : cols.stop // 16])
+        def combine_apart(op, result, left, left_window, left_lists, right, right_window, right_lists, t, cols):
+            for term in range(2):
+                fetch(left[:, term, t, cols], left_window, left_lists[term], cols)
+            for term in range(2):
+                fetch(right[:, term, t, cols], right_window, right_lists[term], cols)
+            nc.vector.tensor_tensor(result[:, :, t, cols], left[:, :, t, cols], right[:, :, t, cols], op)
 
-        def fetch(out, win, lst, cols):
-            nc.scalar.activation(out, at(win, lst, cols), ACT.Copy)
-
-        def woven(ap):
-            return ap.rearrange("p (c i t) -> p c t i", i=4, t=PACK)
-
-        def by_plane(ap):
-            return ap.rearrange("p t (c i) -> p c t i", i=4)
-
-        def pair(spec, g, t, cols, left, right, lists4, got, other, both, op, between=None):
-            how = spec["unf"].get("%d,%d" % (t, g), 0)
-            fetch(got[:, 0, t, cols], left, lists4[0], cols)
-            if between:
-                between()
-            if [t, g] in spec.get("vplain", []):
-                nc.vector.tensor_copy(got[:, 1, t, cols], at(left, lists4[1], cols))
-            else:
-                fetch(got[:, 1, t, cols], left, lists4[1], cols)
-            if how == 2:
-                fetch(other[:, 0, t, cols], right, lists4[2], cols)
-                fetch(other[:, 1, t, cols], right, lists4[3], cols)
-                nc.vector.tensor_tensor(both[:, :, t, cols], got[:, :, t, cols], other[:, :, t, cols], op)
-            else:
-                if how == 1:
-                    fetch(other[:, 1, t, cols], right, lists4[3], cols)
-                nc.vector.tensor_tensor(both[:, 0, t, cols], at(right, lists4[2], cols), got[:, 0, t, cols], op)
-                if how == 1:
-                    nc.vector.tensor_tensor(both[:, 1, t, cols], other[:, 1, t, cols], got[:, 1, t, cols], op)
-                else:
-                    nc.vector.tensor_tensor(both[:, 1, t, cols], at(right, lists4[3], cols), got[:, 1, t, cols], op)
-
-        z_words = sb([P, S], U32, "z_words")
-        z_plane = sb([P, S], U8, "z_plane")
         y_at = sb([P, 2, PACK, S], F32, "y_at")
         d_at = sb([P, 2, PACK, S], F32, "d_at")
         sums = sb([P, 2, PACK, S], F32, "sums")
+        z_words = sb([P, S], U32, "z_words")
+        z_scales = sb([P, S], U8, "z_scales")
 
-        def empty(win, bank, t, on_vector):
-            if on_vector:
-                nc.vector.tensor_scalar_mul(win[:, 0:S], bank[:], gain_abs[:, t : t + 1])
+        def empty_on_scalar(window, bank, t):
+            nc.scalar.activation(window[:, ALL], bank[:], ACT.Copy, scale=gain_abs[:, t : t + 1])
+
+        def lead_sums(t):
+            empty_on_scalar(y[t], y_banks[t], t)
+            fetch(y_at[:, 0, t, lead_cols(t)], y[t], n1_list, lead_cols(t))
+            if t == 0:
+                nc.vector.tensor_scalar_mul(d[t][:, ALL], d_banks[t][:], gain_abs[:, t : t + 1])
             else:
-                nc.scalar.activation(win[:, 0:S], bank[:], ACT.Copy, scale=gain_abs[:, t : t + 1])
+                empty_on_scalar(d[t], d_banks[t], t)
+            fetch(y_at[:, 1, t, lead_cols(t)], y[t], n2_list, lead_cols(t))
+            combine_fused(ALU.add, sums, y_at, d[t], (n3_list, n4_list), t, lead_cols(t))
 
-        def make_h(g):
-            edge = bounds(P1["chunks"])
-            cols = slice(edge[g], edge[g + 1])
-            w = cols.stop - cols.start
-            z_abs = sb([P, PACK * w], BF16, "z_abs_%d" % g)
-            nc.vector.tensor_tensor(woven(z_abs[:]), by_plane(sums[:, 0, :, cols]), by_plane(sums[:, 1, :, cols]), ALU.max)
-            z = sb([P, PACK * w], BF16, "z_%d" % g)
-            nc.vector.tensor_tensor(z[:], z_abs[:], gain_sign[:, 0:w, :].rearrange("p c t -> p (c t)"), ALU.mult)
-            nc.vector.quantize_mx(z_words[:, cols].bitcast(FP8X4), z_plane[:, cols], z[:])
+        def late_sums(t, cols):
+            combine_apart(ALU.add, sums, y_at, y[t], (n1_list, n2_list), d_at, d[t], (n3_list, n4_list), t, cols)
+
+        lead_sums(0)
+        dk_words = pick(d_word_table, k1_list, U32, "dk_words")
+        dk_bytes_dealt = deal_bytes(dk_bytes, "dk_bytes_dealt")
+        dk_dealt = deal_words(nc.vector.tensor_copy, dk_words[:], "dk_dealt")
+        for r in range(4):
+            nc.sync.dma_start(dk_scales[r:P:32, :].bitcast(I32), dk_bytes_dealt[8 * r : P : 32, :].bitcast(I32))
+
+        def make_h(cols, first_bank):
+            name = "_%d" % cols.start
+            z_abs = sb([P, PACK * width(cols)], BF16, "z_abs" + name)
+            nc.vector.tensor_tensor(woven(z_abs[:]), by_row_tile(sums[:, 0, :, cols]), by_row_tile(sums[:, 1, :, cols]), ALU.max)
+            z = sb([P, PACK * width(cols)], BF16, "z" + name)
+            nc.vector.tensor_tensor(z[:], z_abs[:], gain_sign[:, 0 : width(cols), :].rearrange("p c t -> p (c t)"), ALU.mult)
+            nc.vector.quantize_mx(z_words[:, cols].bitcast(FP8X4), z_scales[:, cols], z[:])
             for t in range(PACK):
-                bank = psum.tile([P, S], F32, name="bank%d" % (t + PACK * (g % 2)))
-                product(bank, cols, t, dk_dealt, dk_plane, z_words, z_plane)
-                if cols.stop == S and t > 0:
+                bank = bank_tile(first_bank + t)
+                product(bank, cols, t, dk_dealt, dk_scales, z_words, z_scales)
+                if cols == LAST_QUARTER and t > 0:
                     nc.vector.tensor_scalar_mul(h[t][:, cols], bank[:, cols], H_SCALE)
                 else:
                     nc.scalar.activation(h[t][:, cols], bank[:, cols], ACT.Copy, scale=H_SCALE)
 
-        done = 0
-        empty(y[0], y_banks[0], 0, False)
-        for g, t, cols in plan(P1):
-            for k in range(done, g):
-                make_h(k)
-            done = g
-            if g == 0:
-                if t > 0:
-                    empty(y[t], y_banks[t], t, False)
-            between = (lambda: empty(d[t], d_banks[t], t, t in P1["vev"])) if g == 0 else None
-            pair(P1, g, t, cols, y[t], d[t], (n1_l, n2_l, n3_l, n4_l), y_at, d_at, sums, ALU.add, between)
-        for k in range(done, len(P1["chunks"])):
-            make_h(k)
+        for t in range(1, PACK):
+            lead_sums(t)
+        make_h(FIRST_HALF, 0)
+        late_sums(WHOLE_TILES, SECOND_HALF)
+        late_sums(LAST_TILE, THIRD_QUARTER)
+        make_h(THIRD_QUARTER, PACK)
+        late_sums(LAST_TILE, LAST_QUARTER)
+        make_h(LAST_QUARTER, 0)
 
-        out_rows = out_0.rearrange("(p t) j -> p t j", t=PACK)
+        h_left = sb([P, 2, PACK, S], F32, "h_left")
+        h_right = sb([P, 2, PACK, S], F32, "h_right")
+        products = sb([P, 2, PACK, S], F32, "products")
+        result = sb([P, PACK, S], F32, "result")
         out_words = sb([P, S], I32, "out_words")
-        out_plane = sb([P, S], U8, "out_plane")
-        h_at = sb([P, 2, PACK, S], F32, "h_at", "y_at")
-        h_other = sb([P, 2, PACK, S], F32, "h_other", "d_at")
-        prods = sb([P, 2, PACK, S], F32, "prods")
-        res = sb([P, PACK, S], F32, "res")
+        out_scales = sb([P, S], U8, "out_scales")
+        out_rows = out_0.rearrange("(p t) j -> p t j", t=PACK)
 
-        def hand_on(g):
-            edge = bounds(P2["chunks"])
-            cols = slice(edge[g], edge[g + 1])
-            w = cols.stop - cols.start
-            rounded = sb([P, PACK * w], BF16, "rounded_%d" % g)
-            weave = nc.scalar.copy if g in P2["ilS"] else nc.vector.tensor_copy
-            weave(woven(rounded[:]), by_plane(res[:, :, cols]))
-            nc.vector.quantize_mx(out_words[:, cols].bitcast(FP8X4), out_plane[:, cols], rounded[:])
-            nc.sync.dma_start(as_words(out_1)[:, cols], out_words[:, cols])
+        def subtract(t, cols):
+            nc.vector.tensor_tensor(result[:, t, cols], products[:, 0, t, cols], products[:, 1, t, cols], ALU.subtract)
 
-        for g, t, cols in plan(P2):
-            pair(P2, g, t, cols, h[t], h[t], (n5_l, n7_l, n6_l, n8_l), h_at, h_other, prods, ALU.mult)
-            nc.vector.tensor_tensor(res[:, t, cols], prods[:, 0, t, cols], prods[:, 1, t, cols], ALU.subtract)
-            nc.sync.dma_start(out_rows[:, t, cols], res[:, t, cols])
-        for k in range(len(P2["chunks"])):
-            hand_on(k)
-        for q in range(4):
-            (nc.scalar if q % 2 else nc.sync).dma_start(out_2[0, 4 * q : 4 * q + 4, :].bitcast(I32), out_plane[32 * q : 32 * q + 4, :].bitcast(I32))
+        def store(tiles, cols):
+            nc.sync.dma_start(out_rows[:, tiles, cols], result[:, tiles, cols])
+
+        def late_result(t, cols):
+            combine_apart(ALU.mult, products, h_left, h[t], (n5_list, n7_list), h_right, h[t], (n6_list, n8_list), t, cols)
+            subtract(t, cols)
+
+        def quantise_result(cols, weave):
+            rounded = sb([P, PACK * width(cols)], BF16, "rounded_%d" % cols.start)
+            weave(woven(rounded[:]), by_row_tile(result[:, :, cols]))
+            nc.vector.quantize_mx(out_words[:, cols].bitcast(FP8X4), out_scales[:, cols], rounded[:])
+
+        for t in range(PACK):
+            fetch(h_left[:, 0, t, lead_cols(t)], h[t], n5_list, lead_cols(t))
+            if t == 0:
+                nc.vector.tensor_copy(h_left[:, 1, t, lead_cols(t)], at(h[t], n7_list, lead_cols(t)))
+            else:
+                fetch(h_left[:, 1, t, lead_cols(t)], h[t], n7_list, lead_cols(t))
+            combine_fused(ALU.mult, products, h_left, h[t], (n6_list, n8_list), t, lead_cols(t))
+            subtract(t, lead_cols(t))
+            if t < WHOLE_TILES:
+                store(slice(t, t + 1), ALL)
+        store(slice(WHOLE_TILES, PACK), FIRST_HALF)
+        late_result(WHOLE_TILES, SECOND_HALF)
+        store(slice(WHOLE_TILES, LAST_TILE), SECOND_HALF)
+        late_result(LAST_TILE, THIRD_QUARTER)
+        late_result(LAST_TILE, LAST_QUARTER)
+        store(slice(LAST_TILE, PACK), SECOND_HALF)
+        quantise_result(FIRST_HALF, nc.scalar.copy)
+        nc.sync.dma_start(as_words(out_1)[:, FIRST_HALF], out_words[:, FIRST_HALF])
+        quantise_result(THIRD_QUARTER, nc.scalar.copy)
+        quantise_result(LAST_QUARTER, nc.vector.tensor_copy)
+        nc.sync.dma_start(as_words(out_1)[:, SECOND_HALF], out_words[:, SECOND_HALF])
+        for q in range(QUADRANTS):
+            queue = nc.scalar if q % 2 else nc.sync
+            queue.dma_start(out_2[0, 4 * q : 4 * q + 4, :].bitcast(I32), out_scales[32 * q : 32 * q + 4, :].bitcast(I32))

import math
from contextlib import ExitStack

import concourse.mybir as mybir

K, T, S, H, G = 512, 1024, 512, 512, 2048
FLOPS = 3 * 2 * K * H * S

F32 = mybir.dt.float32
BF16 = mybir.dt.bfloat16
I32 = mybir.dt.int32
U32 = mybir.dt.uint32
U16 = mybir.dt.uint16
U8 = mybir.dt.uint8
FP8X4 = mybir.dt.float8_e4m3fn_x4
ALU = mybir.AluOpType
ACT = mybir.ActivationFunctionType

P = 128
PACK = 4
QUADRANTS = 4
LIST_GROUP = 16
WEAVE_RUN = 4
H_SCALE = 0.0625 * math.sqrt(0.75)

ALL = slice(0, S)
FIRST_HALF = slice(0, S // 2)
SECOND_HALF = slice(S // 2, S)
THIRD_QUARTER = slice(S // 2, 3 * S // 4)
LAST_QUARTER = slice(3 * S // 4, S)
WHOLE_TILES = 2
LAST_TILE = PACK - 1


def width(cols):
    return cols.stop - cols.start


def as_words(dram):
    return dram[0].rearrange("p n r -> p (n r)").bitcast(I32)


def woven(ap):
    return ap.rearrange("p (c i t) -> p c t i", i=WEAVE_RUN, t=PACK)


def by_row_tile(ap):
    return ap.rearrange("p t (c i) -> p c t i", i=WEAVE_RUN)


def tile_picked_twqpathbdet_none_po_kernel(
    tc, x_words, x_scales, w1_words, w1_scales, w2_words, w2_scales, gs, d_words, d_scales,
    offs, two, n1, n2, n3, n4, k1, n5, n6, n7, n8, out_0, out_1, out_2,
):
    nc = tc.nc
    with ExitStack() as ctx:
        lists = ctx.enter_context(tc.tile_pool(name="lists", bufs=1))
        keep = ctx.enter_context(tc.tile_pool(name="keep", bufs=1))
        psum = ctx.enter_context(tc.psum_pool(name="psum", bufs=1))

        def sb(shape, dtype, name):
            return keep.tile(shape, dtype, name=name, align_bytes=64)

        def bank_tile(number):
            return psum.tile([P, S], F32, name="bank%d" % number)

        x_byte_table = sb([P, T], U8, "x_byte_table")
        w1_bytes = sb([P, H], U8, "w1_bytes")
        w2_bytes = sb([P, H], U8, "w2_bytes")
        d_byte_table = sb([P, G], U8, "d_byte_table")
        dk_scales = sb([P, H], U8, "dk_scales")
        for table in (x_byte_table, w1_bytes, w2_bytes):
            nc.gpsimd.memset(table[:].bitcast(I32), 0)
        for table in (d_byte_table, dk_scales):
            nc.vector.memset(table[:].bitcast(I32), 0)

        def load_list(dram, name):
            offsets = lists.tile([P, S // LIST_GROUP], U16, name=name)
            nc.sync.dma_start(offsets[:], dram)
            return offsets

        def load_scale_rows(table, dram):
            for q in range(QUADRANTS):
                nc.sync.dma_start(table[32 * q : 32 * q + 4, :].bitcast(I32), dram[0, 4 * q : 4 * q + 4, :].bitcast(I32))

        def load_words(dram, columns, name):
            table = sb([P, columns], I32, name)
            nc.sync.dma_start(table[:], as_words(dram))
            return table

        gain = sb([P, PACK], F32, "gain")
        nc.gpsimd.dma_start(gain[:], gs.rearrange("(p t) o -> p (t o)", t=PACK))
        nc.gpsimd.dma_start(d_byte_table[0:P:8, :].bitcast(I32), d_scales[0].bitcast(I32))
        x_word_table = load_words(x_words, T, "x_word_table")
        offs_list = load_list(offs, "offs_list")
        load_scale_rows(x_byte_table, x_scales)
        w1_raw = load_words(w1_words, H, "w1_raw")
        w2_raw = load_words(w2_words, H, "w2_raw")
        load_scale_rows(w1_bytes, w1_scales)
        two_list = load_list(two, "two_list")
        n1_list = load_list(n1, "n1_list")
        load_scale_rows(w2_bytes, w2_scales)
        n2_list = load_list(n2, "n2_list")
        n3_list = load_list(n3, "n3_list")
        k1_list = load_list(k1, "k1_list")
        n4_list = load_list(n4, "n4_list")
        d_word_table = load_words(d_words, G, "d_word_table")
        n5_list = load_list(n5, "n5_list")
        n6_list = load_list(n6, "n6_list")
        n7_list = load_list(n7, "n7_list")
        n8_list = load_list(n8, "n8_list")

        def deal_words(copy, words, name):
            dealt = sb([P, H], U32, name)
            copy(dealt[:].rearrange("p (t m) -> p m t", t=PACK), words.rearrange("p (m t) -> p m t", t=PACK))
            return dealt

        def deal_bytes(scale_bytes, name):
            dealt = sb([P, H], U8, name)
            nc.vector.tensor_copy(dealt[:].rearrange("p (t m) -> p t m", t=PACK), scale_bytes[:].rearrange("p (m t) -> p t m", t=PACK))
            return dealt

        def pick(table, offsets, dtype, name):
            picked = sb([P, S], dtype, name)
            nc.vector.tensor_copy(picked[:], table[:].bitcast(dtype).indirect(offsets[:]))
            return picked

        def product(bank, cols, t, stationary, stationary_scales, moving, moving_scales):
            rows = slice(P * t, P * (t + 1))
            nc.tensor.matmul_mx(
                out=bank[:, cols], lhsT=stationary[:, rows].bitcast(FP8X4), lhsT_scale=stationary_scales[:, rows],
                rhs=moving[:, cols].bitcast(FP8X4), rhs_scale=moving_scales[:, cols], start=True, stop=True,
            )

        w1_dealt = deal_words(nc.scalar.copy, w1_raw[:].bitcast(U32), "w1_dealt")
        gain_abs = sb([P, PACK], F32, "gain_abs")
        nc.scalar.activation(gain_abs[:], gain[:], ACT.Abs)
        w2_dealt = deal_words(nc.scalar.copy, w2_raw[:].bitcast(U32), "w2_dealt")
        gain_sign = sb([P, width(FIRST_HALF), PACK], BF16, "gain_sign")
        nc.scalar.activation(gain_sign[:], gain[:].unsqueeze(1).to_broadcast([P, width(FIRST_HALF), PACK]), ACT.Sign)

        x1_scales = pick(x_byte_table, offs_list, U8, "x1_scales")
        x1_words = pick(x_word_table, offs_list, U32, "x1_words")
        w1_dealt_scales = deal_bytes(w1_bytes, "w1_dealt_scales")
        x2_scales = pick(x_byte_table, two_list, U8, "x2_scales")
        x2_words = pick(x_word_table, two_list, U32, "x2_words")
        y_banks = [bank_tile(t) for t in range(PACK)]
        d_banks = [bank_tile(PACK + t) for t in range(PACK)]
        for t in range(PACK):
            product(y_banks[t], ALL, t, w1_dealt, w1_dealt_scales, x1_words, x1_scales)
        w2_dealt_scales = deal_bytes(w2_bytes, "w2_dealt_scales")
        for t in range(PACK):
            product(d_banks[t], ALL, t, w2_dealt, w2_dealt_scales, x2_words, x2_scales)
        dk_bytes = pick(d_byte_table, k1_list, U8, "dk_bytes")

        def windows(name):
            return [sb([P, 2 * S if t < WHOLE_TILES else S], F32, "%s%d" % (name, t)) for t in range(PACK)]

        y, d, h = windows("y"), windows("d"), windows("h")

        def at(window, offsets, cols):
            return window[:].indirect(offsets[:, cols.start // LIST_GROUP : cols.stop // LIST_GROUP])

        def fetch(out, window, offsets, cols):
            nc.scalar.activation(out, at(window, offsets, cols), ACT.Copy)

        def lead_cols(t):
            return ALL if t < WHOLE_TILES else FIRST_HALF

        def combine_fused(op, result, left, right_window, right_lists, t, cols):
            for term in range(2):
                nc.vector.tensor_tensor(result[:, term, t, cols], at(right_window, right_lists[term], cols), left[:, term, t, cols], op)

        def combine_apart(op, result, left, left_window, left_lists, right, right_window, right_lists, t, cols):
            for term in range(2):
                fetch(left[:, term, t, cols], left_window, left_lists[term], cols)
            for term in range(2):
                fetch(right[:, term, t, cols], right_window, right_lists[term], cols)
            nc.vector.tensor_tensor(result[:, :, t, cols], left[:, :, t, cols], right[:, :, t, cols], op)

        y_at = sb([P, 2, PACK, S], F32, "y_at")
        d_at = sb([P, 2, PACK, S], F32, "d_at")
        sums = sb([P, 2, PACK, S], F32, "sums")
        z_words = sb([P, S], U32, "z_words")
        z_scales = sb([P, S], U8, "z_scales")

        def empty_on_scalar(window, bank, t):
            nc.scalar.activation(window[:, ALL], bank[:], ACT.Copy, scale=gain_abs[:, t : t + 1])

        def lead_sums(t):
            empty_on_scalar(y[t], y_banks[t], t)
            fetch(y_at[:, 0, t, lead_cols(t)], y[t], n1_list, lead_cols(t))
            if t == 0:
                nc.vector.tensor_scalar_mul(d[t][:, ALL], d_banks[t][:], gain_abs[:, t : t + 1])
            else:
                empty_on_scalar(d[t], d_banks[t], t)
            fetch(y_at[:, 1, t, lead_cols(t)], y[t], n2_list, lead_cols(t))
            combine_fused(ALU.add, sums, y_at, d[t], (n3_list, n4_list), t, lead_cols(t))

        def late_sums(t, cols):
            combine_apart(ALU.add, sums, y_at, y[t], (n1_list, n2_list), d_at, d[t], (n3_list, n4_list), t, cols)

        lead_sums(0)
        dk_words = pick(d_word_table, k1_list, U32, "dk_words")
        dk_bytes_dealt = deal_bytes(dk_bytes, "dk_bytes_dealt")
        dk_dealt = deal_words(nc.vector.tensor_copy, dk_words[:], "dk_dealt")
        for r in range(4):
            nc.sync.dma_start(dk_scales[r:P:32, :].bitcast(I32), dk_bytes_dealt[8 * r : P : 32, :].bitcast(I32))

        def make_h(cols, first_bank):
            name = "_%d" % cols.start
            z_abs = sb([P, PACK * width(cols)], BF16, "z_abs" + name)
            nc.vector.tensor_tensor(woven(z_abs[:]), by_row_tile(sums[:, 0, :, cols]), by_row_tile(sums[:, 1, :, cols]), ALU.max)
            z = sb([P, PACK * width(cols)], BF16, "z" + name)
            nc.vector.tensor_tensor(z[:], z_abs[:], gain_sign[:, 0 : width(cols), :].rearrange("p c t -> p (c t)"), ALU.mult)
            nc.vector.quantize_mx(z_words[:, cols].bitcast(FP8X4), z_scales[:, cols], z[:])
            for t in range(PACK):
                bank = bank_tile(first_bank + t)
                product(bank, cols, t, dk_dealt, dk_scales, z_words, z_scales)
                if cols == LAST_QUARTER and t > 0:
                    nc.vector.tensor_scalar_mul(h[t][:, cols], bank[:, cols], H_SCALE)
                else:
                    nc.scalar.activation(h[t][:, cols], bank[:, cols], ACT.Copy, scale=H_SCALE)

        for t in range(1, PACK):
            lead_sums(t)
        make_h(FIRST_HALF, 0)
        late_sums(WHOLE_TILES, SECOND_HALF)
        late_sums(LAST_TILE, THIRD_QUARTER)
        make_h(THIRD_QUARTER, PACK)
        late_sums(LAST_TILE, LAST_QUARTER)
        make_h(LAST_QUARTER, 0)

        h_left = sb([P, 2, PACK, S], F32, "h_left")
        h_right = sb([P, 2, PACK, S], F32, "h_right")
        products = sb([P, 2, PACK, S], F32, "products")
        result = sb([P, PACK, S], F32, "result")
        out_words = sb([P, S], I32, "out_words")
        out_scales = sb([P, S], U8, "out_scales")
        out_rows = out_0.rearrange("(p t) j -> p t j", t=PACK)

        def subtract(t, cols):
            nc.vector.tensor_tensor(result[:, t, cols], products[:, 0, t, cols], products[:, 1, t, cols], ALU.subtract)

        def store(tiles, cols):
            nc.sync.dma_start(out_rows[:, tiles, cols], result[:, tiles, cols])

        def late_result(t, cols):
            combine_apart(ALU.mult, products, h_left, h[t], (n5_list, n7_list), h_right, h[t], (n6_list, n8_list), t, cols)
            subtract(t, cols)

        def quantise_result(cols, weave):
            rounded = sb([P, PACK * width(cols)], BF16, "rounded_%d" % cols.start)
            weave(woven(rounded[:]), by_row_tile(result[:, :, cols]))
            nc.vector.quantize_mx(out_words[:, cols].bitcast(FP8X4), out_scales[:, cols], rounded[:])

        for t in range(PACK):
            fetch(h_left[:, 0, t, lead_cols(t)], h[t], n5_list, lead_cols(t))
            if t == 0:
                nc.vector.tensor_copy(h_left[:, 1, t, lead_cols(t)], at(h[t], n7_list, lead_cols(t)))
            else:
                fetch(h_left[:, 1, t, lead_cols(t)], h[t], n7_list, lead_cols(t))
            combine_fused(ALU.mult, products, h_left, h[t], (n6_list, n8_list), t, lead_cols(t))
            subtract(t, lead_cols(t))
            if t < WHOLE_TILES:
                store(slice(t, t + 1), ALL)
        store(slice(WHOLE_TILES, PACK), FIRST_HALF)
        late_result(WHOLE_TILES, SECOND_HALF)
        store(slice(WHOLE_TILES, LAST_TILE), SECOND_HALF)
        late_result(LAST_TILE, THIRD_QUARTER)
        late_result(LAST_TILE, LAST_QUARTER)
        store(slice(LAST_TILE, PACK), SECOND_HALF)
        quantise_result(FIRST_HALF, nc.scalar.copy)
        nc.sync.dma_start(as_words(out_1)[:, FIRST_HALF], out_words[:, FIRST_HALF])
        quantise_result(THIRD_QUARTER, nc.scalar.copy)
        quantise_result(LAST_QUARTER, nc.vector.tensor_copy)
        nc.sync.dma_start(as_words(out_1)[:, SECOND_HALF], out_words[:, SECOND_HALF])
        for q in range(QUADRANTS):
            queue = nc.scalar if q % 2 else nc.sync
            queue.dma_start(out_2[0, 4 * q : 4 * q + 4, :].bitcast(I32), out_scales[32 * q : 32 * q + 4, :].bitcast(I32))
